import numpy as np
import ml_dtypes


def mxq(x, axis, fmt="e4m3"):
    dtype, down = {"e4m3": (ml_dtypes.float8_e4m3fn, 7), "e5m2": (ml_dtypes.float8_e5m2, 14)}[fmt]
    v = np.moveaxis(np.asarray(x, np.float32).astype(ml_dtypes.bfloat16).astype(np.float64), axis, -1)
    blocks = v.reshape(v.shape[:-1] + (-1, 32))
    amax = np.abs(blocks).max(-1, keepdims=True)
    byte = np.maximum(np.where(amax > 0, np.frexp(amax)[1] - 1 + 127, 0) - down, 1)
    scale = np.exp2(byte - 127.0)
    codes = (blocks / scale).astype(np.float32).astype(dtype).astype(np.float64)
    return np.moveaxis((codes * scale).reshape(v.shape), -1, axis)


WIDE = False


def mx_kscale(k):
    if not WIDE:
        return np.ones(k)
    levels = np.array([10, -10, 5, -5, 0])
    if k % 512:
        return np.exp2(np.random.permutation(np.resize(levels, k // 32))).repeat(32)
    a = np.empty((k // 512, 16))
    for p in range(k // 512):
        a[p, :8] = np.random.permutation(np.resize(levels, 8))
        for g in range(8):
            far = levels[np.abs(levels - a[p, g]) >= 10]
            a[p, g + 8] = far[np.random.randint(len(far))]
    return np.exp2(a.ravel()).repeat(32)


def f64(x):
    return np.asarray(x).astype(np.float64)


def striped(idx):
    return np.tile(idx.reshape(-1, 16).T, (8, 1)).astype(np.uint16)


def unstriped(offs):
    return offs[:16].T.reshape(-1).astype(np.int64)


def sigmoid(v):
    return 1.0 / (1.0 + np.exp(-np.maximum(v, -700.0)))


def d_sigmoid(v):
    s = 1.0 / (1.0 + np.exp(-np.maximum(v, -700.0)))
    return s * (1.0 - s)


K, T, E, C, H, N = 128, 768, 12, 128, 512, 1024


def by_expert(wq, xq):
    return np.concatenate([wq[e].T @ xq[:, e * C:(e + 1) * C] for e in range(E)], axis=1)


def setup_inputs():
    n = np.random.standard_normal
    s = mx_kscale(N)[:, None]
    u = mx_kscale(H)
    first = np.random.permutation(np.repeat(np.arange(E), T // E))
    second = (first + 1 + np.random.permutation(np.repeat(np.arange(E - 1), -(-T // (E - 1)))[:T])) % E
    while np.bincount(second, minlength=E).max() != T // E:
        load = np.bincount(second, minlength=E); hi, lo = int(load.argmax()), int(load.argmin())
        t = np.flatnonzero((second == hi) & (first != lo))[0]; second[t] = lo
    slot_token = np.empty(E * C, np.int64); pos = np.empty((2, T), np.int64); fill = np.zeros(E, np.int64)
    place = np.stack([np.random.permutation(C) for _ in range(E)])
    for r, deal in enumerate((first, second)):
        for t in np.random.permutation(T):
            e = deal[t]; j = e * C + place[e, fill[e]]; fill[e] += 1; slot_token[j] = t; pos[r, t] = j
    g = np.random.uniform(0.2, 0.8, T)
    w_slot = np.empty(E * C); w_slot[pos[0]] = g; w_slot[pos[1]] = 1.0 - g
    return {
        "dyT": (n((N, T)) * s).astype(np.float32),
        "a1": n((H, E * C)).astype(np.float32),
        "a3": n((H, E * C)).astype(np.float32),
        "w2": (n((E, N, H)) / np.sqrt(N) / s[None] * u[None, None, :]).astype(np.float32),
        "w1": (n((E, H, K)) / np.sqrt(H) / u[None, :, None]).astype(np.float32),
        "w3": (n((E, H, K)) / np.sqrt(H) / u[None, :, None]).astype(np.float32),
        "gate": np.tile(w_slot, (N, 1)).astype(np.float32),
        "offs": striped(slot_token),
        "pos1": striped(pos[0]),
        "pos2": striped(pos[1]),
    }


def reference(dyT, a1, a3, w2, w1, w3, gate, offs, pos1, pos2):
    idx = unstriped(offs)
    gq = mxq(f64(gate) * f64(dyT)[:, idx], 0, "e4m3")
    dh = by_expert(mxq(f64(w2), 1, "e4m3"), gq)
    da1 = dh * f64(a3) * d_sigmoid(f64(a1))
    da3 = dh * sigmoid(f64(a1))
    dx = by_expert(mxq(f64(w1), 1, "e4m3"), mxq(da1, 0, "e4m3")) + by_expert(mxq(f64(w3), 1, "e4m3"), mxq(da3, 0, "e4m3"))
    return dx[:, unstriped(pos1)] + dx[:, unstriped(pos2)]

from contextlib import ExitStack

import concourse.mybir as mybir

K, T, E, C, H, N = 128, 768, 12, 128, 512, 1024
P = 128
SLOTS = E * C
GROUP = 4
GC = GROUP * C
NG = E // GROUP
PASSES = N // 512

FLOPS = 2 * SLOTS * (N * H + 2 * H * K)
BYTES = 4 * (N * T + 2 * H * SLOTS + E * N * H + 2 * E * H * K + P * SLOTS + K * T)

F32 = mybir.dt.float32
BF16 = mybir.dt.bfloat16
U32 = mybir.dt.uint32
U16 = mybir.dt.uint16
U8 = mybir.dt.uint8
FP8X4 = mybir.dt.float8_e4m3fn_x4
ALU = mybir.AluOpType
ACT = mybir.ActivationFunctionType


def tile_moe_bdx_glu_sigmoid_kernel(
    tc, dyT, a1, a3, w2, w1, w3, gate, offs, pos1, pos2, out
):
    nc = tc.nc
    with ExitStack() as ctx:
        lists = ctx.enter_context(tc.tile_pool(name="lists", bufs=1))
        keep = ctx.enter_context(tc.tile_pool(name="keep", bufs=1))
        two = ctx.enter_context(tc.tile_pool(name="two", bufs=2))
        three = ctx.enter_context(tc.tile_pool(name="three", bufs=3))
        five = ctx.enter_context(tc.tile_pool(name="five", bufs=5))
        psum = ctx.enter_context(tc.psum_pool(name="psum", bufs=4))

        offs_sb = lists.tile([P, SLOTS // 16], U16, name="offs_sb")
        pos1_sb = lists.tile([P, T // 16], U16, name="pos1_sb")
        pos2_sb = lists.tile([P, T // 16], U16, name="pos2_sb")

        dy = {}
        gates = {}
        w2_raw = {}
        w13_raw = {}
        a_raw = {}
        dy_view = dyT.rearrange("(g p t) c -> g t p c", p=P, t=4)

        def load_dy(g, t):
            dy[g, t] = keep.tile([P, T], F32, name=f"dy{g}{t}")
            nc.sync.dma_start(out=dy[g, t][:], in_=dy_view[g, t])

        def load_gate(q):
            gates[q] = keep.tile([P, GC], F32, name=f"gate{q}")
            nc.sync.dma_start(out=gates[q][:], in_=gate[0:P, q * GC : (q + 1) * GC])

        def load_w2(e, g):
            raw = five.tile([P, 4, H], F32, name="w2_raw")
            nc.sync.dma_start(
                out=raw[:], in_=w2[e, g * 512 : (g + 1) * 512, :].rearrange("(p j) i -> p j i", j=4)
            )
            w2_raw[e, g] = raw

        def load_w13(e):
            for which, w in ((0, w1), (1, w3)):
                raw = two.tile([P, 2, 4 * K], F32, name=f"w13_raw{which}")
                nc.sync.dma_start(
                    out=raw[:], in_=w[e : e + 2].rearrange("e (p j) k -> p e (j k)", j=4)
                )
                for d in (0, 1):
                    w13_raw[e + d, which] = raw[:, d, :]

        def load_a(q):
            for which, a in ((1, a1), (3, a3)):
                raw = two.tile([P, 4, GC], F32, name=f"a{which}_raw")
                nc.sync.dma_start(
                    out=raw[:],
                    in_=a[:, q * GC : (q + 1) * GC].rearrange("(p t) c -> p t c", t=4),
                )
                a_raw[q, which] = raw

        g_f32 = {}
        g_bf = {}
        g_codes = {}
        g_scales = {}

        def gather(q, g, t):
            if t == 0:
                g_f32[q, g] = three.tile([P, 4, GC], F32, name="g_f32")
            nc.vector.tensor_tensor(
                out=g_f32[q, g][:, t, :],
                in0=dy[g, t][:].indirect(offs_sb[:, q * GC // 16 : (q + 1) * GC // 16]),
                in1=gates[q][:],
                op=ALU.mult,
            )

        def pack_g(q, g):
            g_bf[q, g] = two.tile([P, 4 * GC], BF16, name="g_bf", align_bytes=64)
            nc.scalar.copy(
                out=g_bf[q, g][:].rearrange("p (c i t) -> p c t i", i=4, t=4),
                in_=g_f32[q, g][:].rearrange("p t (c i) -> p c t i", i=4),
            )

        def quant_g(q, g):
            g_codes[q, g] = keep.tile([P, GC], U32, name=f"g_codes{q}{g}", align_bytes=64)
            g_scales[q, g] = keep.tile([P, GC], U8, name=f"g_scales{q}{g}", align_bytes=64)
            nc.vector.quantize_mx(
                out=g_codes[q, g][:].bitcast(FP8X4), scales=g_scales[q, g][:], in_=g_bf[q, g][:]
            )

        w2_bf = {}
        w2_codes = {}
        w2_scales = {}

        def pack_w2(e, g):
            w2_bf[e, g] = three.tile([P, 4 * H], BF16, name="w2_bf", align_bytes=64)
            nc.scalar.copy(
                out=w2_bf[e, g][:].rearrange("p (t m j) -> p m j t", t=4, j=4),
                in_=w2_raw[e, g][:].rearrange("p j (m t) -> p m j t", t=4),
            )

        def quant_w2(e, g):
            w2_codes[e, g] = five.tile([P, H], U32, name="w2_codes", align_bytes=64)
            w2_scales[e, g] = five.tile([P, H], U8, name="w2_scales", align_bytes=64)
            nc.vector.quantize_mx(
                out=w2_codes[e, g][:].bitcast(FP8X4), scales=w2_scales[e, g][:], in_=w2_bf[e, g][:]
            )

        w13_bf = {}
        w13_codes = {}
        w13_scales = {}

        def pack_w13(e):
            w13_bf[e] = two.tile([P, 2, 4 * K], BF16, name="w13_bf", align_bytes=64)
            for which in (0, 1):
                nc.vector.tensor_copy(
                    out=w13_bf[e][:, which, :].rearrange("p (c i j) -> p c j i", i=4, j=4),
                    in_=w13_raw[e, which].rearrange("p (j c i) -> p c j i", j=4, i=4),
                )

        def quant_w13(e):
            w13_codes[e] = three.tile([P, 2 * K], U32, name="w13_codes", align_bytes=64)
            w13_scales[e] = three.tile([P, 2 * K], U8, name="w13_scales", align_bytes=64)
            nc.vector.quantize_mx(
                out=w13_codes[e][:].bitcast(FP8X4),
                scales=w13_scales[e][:],
                in_=w13_bf[e][:].rearrange("p s x -> p (s x)"),
            )

        def sigmoid(q):
            s = a_raw[q, 1]
            nc.scalar.activation(out=s[:], in_=s[:], func=ACT.Sigmoid)

        def slope(q):
            s = a_raw[q, 1]
            r = a_raw[q, 3]
            nc.vector.scalar_tensor_tensor(
                out=r[:], in0=s[:], scalar=1.0, in1=r[:], op0=ALU.subtract, op1=ALU.mult
            )

        dh = {}

        def first(e):
            q, c0 = e // GROUP, (e % GROUP) * C
            dh[e] = psum.tile([P, 4, C], F32, name="dh")
            for t in range(4):
                for g in range(PASSES):
                    nc.tensor.matmul_mx(
                        out=dh[e][:, t, :],
                        lhsT=w2_codes[e, g][:, t * P : (t + 1) * P].bitcast(FP8X4),
                        lhsT_scale=w2_scales[e, g][:, t * P : (t + 1) * P],
                        rhs=g_codes[q, g][:, c0 : c0 + C].bitcast(FP8X4),
                        rhs_scale=g_scales[q, g][:, c0 : c0 + C],
                        start=(g == 0),
                        stop=(g == PASSES - 1),
                    )

        da_f32 = {}
        da_bf = {}
        da_codes = {}
        da_scales = {}

        def da_first(e):
            q, c0 = e // GROUP, (e % GROUP) * C
            da_f32[e] = three.tile([P, 4, C], F32, name="da_f32")
            da_bf[e] = two.tile([P, 2, 4 * C], BF16, name="da_bf", align_bytes=64)
            nc.vector.scalar_tensor_tensor(
                out=da_f32[e][:],
                in0=dh[e][:],
                scalar=-1.0,
                in1=a_raw[q, 1][:, :, c0 : c0 + C],
                op0=ALU.mult,
                op1=ALU.mult,
            )
            nc.scalar.activation(
                out=da_bf[e][:, 1, :].rearrange("p (c i t) -> p c t i", i=4, t=4),
                in_=da_f32[e][:].rearrange("p t (c i) -> p c t i", i=4),
                func=ACT.Copy,
                scale=-1.0,
            )

        def da_second(e):
            q, c0 = e // GROUP, (e % GROUP) * C
            nc.vector.tensor_tensor(
                out=da_bf[e][:, 0, :].rearrange("p (c i t) -> p c t i", i=4, t=4),
                in0=da_f32[e][:].rearrange("p t (c i) -> p c t i", i=4),
                in1=a_raw[q, 3][:, :, c0 : c0 + C].rearrange("p t (c i) -> p c t i", i=4),
                op=ALU.mult,
            )

        def quant_da(e):
            da_codes[e] = two.tile([P, 2 * C], U32, name="da_codes", align_bytes=64)
            da_scales[e] = two.tile([P, 2 * C], U8, name="da_scales", align_bytes=64)
            nc.vector.quantize_mx(
                out=da_codes[e][:].bitcast(FP8X4),
                scales=da_scales[e][:],
                in_=da_bf[e][:].rearrange("p s x -> p (s x)"),
            )

        dxs = {}
        dx_all = keep.tile([P, SLOTS], F32, name="dx_all")

        def second(e):
            dx = psum.tile([P, C], F32, name="dx")
            for s in (0, 1):
                cols = slice(s * C, (s + 1) * C)
                nc.tensor.matmul_mx(
                    out=dx[:],
                    lhsT=w13_codes[e][:, cols].bitcast(FP8X4),
                    lhsT_scale=w13_scales[e][:, cols],
                    rhs=da_codes[e][:, cols].bitcast(FP8X4),
                    rhs_scale=da_scales[e][:, cols],
                    start=(s == 0),
                    stop=(s == 1),
                )
            dxs[e] = dx

        def dx_copy(e):
            nc.scalar.copy(out=dx_all[:, e * C : (e + 1) * C], in_=dxs[e][:])

        nc.sync.dma_start(out=offs_sb[:], in_=offs)
        load_dy(0, 0)
        load_gate(0)
        load_w2(0, 0)
        for t in (1, 2, 3):
            load_dy(0, t)
        load_w2(0, 1)
        for t in range(4):
            load_dy(1, t)
        load_a(0)
        load_gate(1)
        load_w2(1, 0)
        load_w2(1, 1)
        load_w13(0)
        load_w2(2, 0)
        load_w2(2, 1)
        load_gate(2)

        pack_w2(0, 0)
        for t in range(4):
            gather(0, 0, t)
        quant_w2(0, 0)
        pack_g(0, 0)
        pack_w2(0, 1)
        for t in range(4):
            gather(0, 1, t)
        quant_g(0, 0)
        quant_w2(0, 1)
        sigmoid(0)
        pack_g(0, 1)
        gather(1, 0, 0)
        pack_w2(1, 0)
        quant_g(0, 1)
        first(0)
        gather(1, 0, 1)
        pack_w2(1, 1)
        slope(0)
        gather(1, 0, 2)
        quant_w2(1, 0)
        gather(1, 0, 3)
        quant_w2(1, 1)
        first(1)
        pack_w13(0)
        quant_w13(0)
        pack_g(1, 0)
        pack_w2(2, 0)
        pack_w2(2, 1)
        quant_g(1, 0)


        for e in range(E + 1):
            if e + 3 < E:
                load_w2(e + 3, 0)
                load_w2(e + 3, 1)
            if e % 2 == 0 and e + 2 < E:
                load_w13(e + 2)
            if e in (0, 4):
                load_a(e // 4 + 1)
            if e == 2:
                nc.sync.dma_start(out=pos1_sb[:], in_=pos1)
                nc.sync.dma_start(out=pos2_sb[:], in_=pos2)
            if e < E:
                da_first(e)
            if e + 2 < E:
                quant_w2(e + 2, 0)
            if e > 0:
                quant_da(e - 1)
                second(e - 1)
            if e < E:
                da_second(e)
            if e + 3 < E:
                pack_w2(e + 3, 0)
            if e + 2 < E:
                quant_w2(e + 2, 1)
            if e + 2 < E and (e + 2) % 4 != 0:
                first(e + 2)
            if e > 0:
                dx_copy(e - 1)
            if e + 1 < E:
                pack_w13(e + 1)
                quant_w13(e + 1)
            if e + 3 < E:
                pack_w2(e + 3, 1)
            if e == 0:
                gather(1, 1, 0)
                gather(1, 1, 1)
            if e == 1:
                gather(1, 1, 2)
                gather(1, 1, 3)
                pack_g(1, 1)
            if e == 2:
                quant_g(1, 1)
                first(4)
                sigmoid(1)
            if e in (2, 3, 4, 5):
                gather(2, (e - 2) // 2, 2 * (e % 2))
                gather(2, (e - 2) // 2, 2 * (e % 2) + 1)
            if e == 3:
                pack_g(2, 0)
                slope(1)
            if e == 4:
                quant_g(2, 0)
            if e == 5:
                pack_g(2, 1)
            if e == 6:
                quant_g(2, 1)
                first(8)
                sigmoid(2)
            if e == 7:
                slope(2)
        picked = [keep.tile([P, T], F32, name=f"picked{r}") for r in (0, 1)]
        nc.vector.tensor_copy(out=picked[0][:], in_=dx_all[:].indirect(pos1_sb[:]))
        nc.vector.tensor_copy(out=picked[1][:], in_=dx_all[:].indirect(pos2_sb[:]))
        total = keep.tile([P, T], F32, name="total")
        nc.vector.tensor_add(out=total[:], in0=picked[0][:], in1=picked[1][:])
        nc.sync.dma_start(out=out, in_=total[:])
